import numpy as np
import ml_dtypes


def mxq(x, axis, fmt="e4m3"):
    dtype, down = {"e4m3": (ml_dtypes.float8_e4m3fn, 7), "e5m2": (ml_dtypes.float8_e5m2, 14)}[fmt]
    v = np.moveaxis(np.asarray(x, np.float32).astype(ml_dtypes.bfloat16).astype(np.float64), axis, -1)
    blocks = v.reshape(v.shape[:-1] + (-1, 32))
    amax = np.abs(blocks).max(-1, keepdims=True)
    byte = np.maximum(np.where(amax > 0, np.frexp(amax)[1] - 1 + 127, 0) - down, 1)
    scale = np.exp2(byte - 127.0)
    codes = (blocks / scale).astype(np.float32).astype(dtype).astype(np.float64)
    return np.moveaxis((codes * scale).reshape(v.shape), -1, axis)


WIDE = False


def mx_kscale(k):
    if not WIDE:
        return np.ones(k)
    levels = np.array([10, -10, 5, -5, 0])
    if k % 512:
        return np.exp2(np.random.permutation(np.resize(levels, k // 32))).repeat(32)
    a = np.empty((k // 512, 16))
    for p in range(k // 512):
        a[p, :8] = np.random.permutation(np.resize(levels, 8))
        for g in range(8):
            far = levels[np.abs(levels - a[p, g]) >= 10]
            a[p, g + 8] = far[np.random.randint(len(far))]
    return np.exp2(a.ravel()).repeat(32)


def f64(x):
    return np.asarray(x).astype(np.float64)


def striped(idx):
    return np.tile(idx.reshape(-1, 16).T, (8, 1)).astype(np.uint16)


def unstriped(offs):
    return offs[:16].T.reshape(-1).astype(np.int64)


def striped8(idx):
    return np.concatenate([x.reshape(-1, 16).T for x in idx]).astype(np.uint16)


def runs(offs, k):
    lists = np.stack([offs[16 * r : 16 * r + 16].T.reshape(-1) for r in range(8)]).astype(np.int64)
    return lists[np.arange(k) % 512 // 64]


def pack_weight(w):
    k, n = w.shape
    w = f64(np.asarray(w, np.float32).astype(ml_dtypes.bfloat16)).reshape(k // 32, 32, n)
    amax = np.abs(w).max(1)
    byte = np.clip(np.where(amax > 0, np.frexp(amax)[1] - 1 + 127 - 7, 1), 1, 254)
    scaled = (w * np.exp2(127.0 - byte)[:, None, :]).reshape(k, n).astype(np.float32)
    words = np.ascontiguousarray(scaled.reshape(k // 512, 128, 4, n).transpose(0, 1, 3, 2)).astype(ml_dtypes.float8_e4m3fn).view(np.uint8)
    return words, np.ascontiguousarray(byte.astype(np.uint8).reshape(k // 512, 16, n))


def unpack_weight(words, scales):
    g, p, n, _ = words.shape
    vals = np.ascontiguousarray(words).view(ml_dtypes.float8_e4m3fn).astype(np.float64) * np.repeat(np.exp2(scales.astype(np.float64) - 127.0), 8, axis=1)[..., None]
    return vals.transpose(0, 1, 3, 2).reshape(g * 512, n)

def planes(y):
    n, m = y.shape
    v = y.astype(np.float32).astype(ml_dtypes.bfloat16).astype(np.float64).reshape(n // 32, 32, m)
    top = np.abs(v).max(1)
    byte = np.clip(np.where(top > 0, np.frexp(top)[1] - 1 + 127 - 7, 1), 1, 254)
    codes = (v * np.exp2(127.0 - byte)[:, None, :]).reshape(n, m).astype(np.float32).astype(ml_dtypes.float8_e4m3fn).view(np.uint8)
    words = codes.reshape(n // 512, 128, 4, m).transpose(0, 1, 3, 2)
    return np.ascontiguousarray(words), np.ascontiguousarray(byte.astype(np.uint8).reshape(n // 512, 16, m))


K, T, S, G, H = 512, 1024, 512, 2048, 512


def setup_inputs():
    n = np.random.standard_normal
    s = mx_kscale(K)[:, None]
    packed_xT = pack_weight(n((K, T)) * s)
    packed_dT = pack_weight(n((K, G)) / s)
    return {
        "x_words": packed_xT[0],
        "x_scales": packed_xT[1],
        "d_words": packed_dT[0],
        "d_scales": packed_dT[1],
        "gs": (np.random.uniform(0.5, 1.5, (K, 1)) * s).astype(np.float32),
        "offs": striped(np.random.permutation(T)[:S]),
        "k1": striped8(np.random.randint(0, G, (8, H))),
        "n1": striped8(np.stack([np.random.permutation(S) for _ in range(8)])),
        "n2": striped8(np.stack([np.random.permutation(S) for _ in range(8)])),
        "k2": striped8(np.random.randint(0, G, (8, H))),
        "n3": striped8(np.stack([np.random.permutation(S) for _ in range(8)])),
        "n4": striped8(np.stack([np.random.permutation(S) for _ in range(8)])),
    }


def reference(x_words, x_scales, d_words, d_scales, gs, offs, k1, n1, n2, k2, n3, n4):
    d_k2 = unpack_weight(d_words, d_scales)[np.arange(K)[:, None], runs(k2, K)]
    d_k1 = unpack_weight(d_words, d_scales)[np.arange(K)[:, None], runs(k1, K)]
    xq = unpack_weight(x_words, x_scales)[:, unstriped(offs)]
    h = 0.0625 * (d_k1.T @ xq)
    ex = np.exp(0.5 * h)
    z = f64(gs) * ((2.0 * ex) / (ex + ex[np.arange(H)[:, None], runs(n1, H)] + ex[np.arange(H)[:, None], runs(n2, H)]))
    h2 = 0.0625 * ((d_k2.T @ mxq(z, 0, "e4m3")))
    st = np.maximum(h2, h2[np.arange(H)[:, None], runs(n3, H)])
    out_0 = np.minimum(st, st[np.arange(H)[:, None], runs(n4, H)])
    return (out_0,) + planes(out_0)

@@ -1,0 +1,216 @@
+from contextlib import ExitStack
+
+import concourse.mybir as mybir
+from concourse.masks import make_identity
+
+F32 = mybir.dt.float32
+BF16 = mybir.dt.bfloat16
+I32 = mybir.dt.int32
+U32 = mybir.dt.uint32
+U16 = mybir.dt.uint16
+U8 = mybir.dt.uint8
+FP8X4 = mybir.dt.float8_e4m3fn_x4
+ACT = mybir.ActivationFunctionType
+ALU = mybir.AluOpType
+
+P = 128
+PACK = 4
+S = 512
+T = 1024
+G = 2048
+HALF = 256
+BLK = 128
+FLOPS = 2 * 2 * 512 * 512 * 512
+
+
+def tile_picked_codesharehopmn_none_po_kernel(tc, x_words, x_scales, d_words, d_scales, gs, offs, k1, n1, n2, k2, n3, n4, out_0, out_1, out_2):
+    nc = tc.nc
+    with ExitStack() as ctx:
+        held = ctx.enter_context(tc.tile_pool(name="held", bufs=1))
+        ring = ctx.enter_context(tc.tile_pool(name="ring", bufs=2))
+        mm_ps = ctx.enter_context(tc.psum_pool(name="mm_ps", bufs=4))
+        den_ps = ctx.enter_context(tc.psum_pool(name="den_ps", bufs=2))
+        back_ps = ctx.enter_context(tc.psum_pool(name="back_ps", bufs=2))
+
+        def load_list(name, src):
+            tile = held.tile([P, S // 16], U16, name=name)
+            nc.sync.dma_start(tile[:], src)
+            return tile
+
+        def entries(lst, lo, hi):
+            return lst[:, lo // 16 : hi // 16]
+
+        def gather(engine, out, window, lst, lo, hi):
+            src = window[:].indirect(entries(lst, lo, hi))
+            if engine == "s":
+                nc.scalar.activation(out=out, in_=src, func=ACT.Copy)
+            else:
+                nc.vector.tensor_copy(out=out, in_=src)
+
+        dw = held.tile([P, G], I32, name="dw", align_bytes=64)
+        ds = held.tile([P, G], U8, name="ds", align_bytes=64)
+        xw = held.tile([P, T], I32, name="xw", align_bytes=64)
+        xs = held.tile([P, T], U8, name="xs", align_bytes=64)
+        nc.gpsimd.memset(ds[:].bitcast(I32), 0)
+        nc.gpsimd.memset(xs[:].bitcast(I32), 0)
+
+        l_k1 = load_list("l_k1", k1)
+        d_rows = d_scales[0].bitcast(I32)
+        for e in range(2):
+            nc.scalar.dma_start(ds[:].bitcast(I32)[e:P:16, :], d_rows[e:16:2, :])
+        l_offs = load_list("l_offs", offs)
+        nc.sync.dma_start(dw[:], d_words[0].rearrange("p n t -> p (n t)").bitcast(I32))
+        nc.sync.dma_start(xw[:], x_words[0].rearrange("p n t -> p (n t)").bitcast(I32))
+        x_rows = x_scales[0].bitcast(I32)
+        for j in range(4):
+            nc.scalar.dma_start(xs[:].bitcast(I32)[j:P:32, :], x_rows[j:16:4, :])
+        gs_t = held.tile([P, PACK], F32, name="gs_t")
+        nc.sync.dma_start(gs_t[:], gs.rearrange("(p t) o -> p (t o)", t=PACK))
+        l_n1 = load_list("l_n1", n1)
+        l_n2 = load_list("l_n2", n2)
+        l_k2 = load_list("l_k2", k2)
+        l_n3 = load_list("l_n3", n3)
+        l_n4 = load_list("l_n4", n4)
+
+        ident = held.tile([P, P], F32, name="ident")
+        make_identity(nc, ident[:])
+
+        def weight_scales(tag, lst, queue):
+            got = held.tile([P, S], U8, name=tag + "_sg", align_bytes=64)
+            nc.vector.tensor_copy(out=got[:], in_=ds[:].indirect(lst[:]))
+            dealt = held.tile([P, S], U8, name=tag + "_sd", align_bytes=64)
+            nc.vector.tensor_copy(out=dealt[:].rearrange("p (t m) -> p m t", t=PACK), in_=got[:].rearrange("p (m t) -> p m t", t=PACK))
+            rows = dealt[:].bitcast(I32)
+            for e in range(2):
+                queue.dma_start(rows[2 + e : P : 32, :], rows[16 + e : P : 32, :])
+            return dealt
+
+        def weight_words(tag, lst, slot):
+            got = held.tile([P, S], I32, name=tag + "_wg", tag=slot, align_bytes=64)
+            nc.vector.tensor_copy(out=got[:].bitcast(U32), in_=dw[:].bitcast(U32).indirect(lst[:]))
+            dealt = held.tile([P, S], I32, name=tag + "_wd", align_bytes=64)
+            nc.vector.tensor_copy(out=dealt[:].rearrange("p (t m) -> p m t", t=PACK), in_=got[:].rearrange("p (m t) -> p m t", t=PACK))
+            return dealt
+
+        w1s = weight_scales("w1", l_k1, nc.scalar)
+        w1w = weight_words("w1", l_k1, "w1_wg")
+
+        xgw = held.tile([P, S], I32, name="xgw", tag="xgw", align_bytes=64)
+        xgs = held.tile([P, S], U8, name="xgs", align_bytes=64)
+        ex = [held.tile([P, S], F32, name="ex%d" % t) for t in range(PACK)]
+        exg = held.tile([P, PACK, S], F32, name="exg")
+        h_ps = [mm_ps.tile([P, S], F32, name="h_ps", tag="mm") for t in range(PACK)]
+        for lo in range(0, S, HALF):
+            hi = lo + HALF
+            nc.vector.tensor_copy(out=xgs[:, lo:hi], in_=xs[:].indirect(entries(l_offs, lo, hi)))
+            nc.vector.tensor_copy(out=xgw[:, lo:hi].bitcast(U32), in_=xw[:].bitcast(U32).indirect(entries(l_offs, lo, hi)))
+            for t in range(PACK):
+                cols = slice(t * P, (t + 1) * P)
+                nc.tensor.matmul_mx(out=h_ps[t][:, lo:hi], lhsT=w1w[:, cols].bitcast(FP8X4), lhsT_scale=w1s[:, cols],
+                                    rhs=xgw[:, lo:hi].bitcast(FP8X4), rhs_scale=xgs[:, lo:hi], start=True, stop=True)
+                nc.scalar.activation(out=ex[t][:, lo:hi], in_=h_ps[t][:, lo:hi], func=ACT.Exp, scale=0.5 * 0.0625)
+        for t in range(PACK):
+            nc.gpsimd.tensor_scalar(out=exg[:, t, :], in0=ex[t][:], scalar1=gs_t[:, t : t + 1], scalar2=0.0, op0=ALU.mult, op1=ALU.add)
+
+        w2s = weight_scales("w2", l_k2, nc.sync)
+
+        e1 = [held.tile([P, S], F32, name="e1_%d" % t) for t in range(PACK)]
+        e2 = [held.tile([P, S], F32, name="e2_%d" % t) for t in range(PACK)]
+        zw = held.tile([P, S], I32, name="zw", align_bytes=64)
+        zs = held.tile([P, S], U8, name="zs", align_bytes=64)
+        h2_ps = [mm_ps.tile([P, S], F32, name="h2_ps", tag="mm") for t in range(PACK)]
+        h2 = [held.tile([P, S], F32, name="h2_%d" % t) for t in range(PACK)]
+
+        def fetch_ex(lo, hi, on_scalar):
+            for t in range(PACK):
+                for which, (dst, lst) in enumerate(((e1, l_n1), (e2, l_n2))):
+                    gather("s" if (t, which) in on_scalar else "v", dst[t][:, lo:hi], ex[t], lst, lo, hi)
+
+        def add_up(blocks):
+            dens = [den_ps.tile([P, PACK, BLK], F32, name="den") for lo in blocks]
+            for t in range(PACK):
+                for den, lo in zip(dens, blocks):
+                    for n, src in enumerate((ex, e1, e2)):
+                        nc.tensor.matmul(den[:, t, :], src[t][:, lo : lo + BLK], ident[:], start=(n == 0), stop=(n == 2), is_transpose=True)
+            return dens
+
+        def invert(den):
+            root_t = ring.tile([P, PACK, BLK], F32, name="root_t")
+            nc.scalar.activation(out=root_t[:], in_=den[:], func=ACT.Abs_reciprocal_sqrt, scale=0.5)
+            inv_t = ring.tile([P, PACK, BLK], F32, name="inv_t")
+            nc.scalar.activation(out=inv_t[:], in_=root_t[:], func=ACT.Square)
+            inv = back_ps.tile([P, PACK, BLK], F32, name="inv")
+            for t in range(PACK):
+                nc.tensor.transpose(inv[:, t, :], inv_t[:, t, :], ident[:])
+            return inv
+
+        def share(lo, inv):
+            blk = slice(lo, lo + BLK)
+            zb = ring.tile([P, BLK * PACK], BF16, name="zb", align_bytes=64)
+            nc.vector.tensor_tensor(out=zb[:].rearrange("p (c i t) -> p c t i", i=4, t=PACK),
+                                    in0=exg[:, :, blk].rearrange("p t (c i) -> p c t i", i=4),
+                                    in1=inv[:].rearrange("p t (c i) -> p c t i", i=4), op=ALU.mult)
+            nc.vector.quantize_mx(out=zw[:, blk].bitcast(FP8X4), scales=zs[:, blk], in_=zb[:])
+
+        def second(lo, w2w):
+            blk = slice(lo, lo + BLK)
+            for t in range(PACK):
+                cols = slice(t * P, (t + 1) * P)
+                nc.tensor.matmul_mx(out=h2_ps[t][:, blk], lhsT=w2w[:, cols].bitcast(FP8X4), lhsT_scale=w2s[:, cols],
+                                    rhs=zw[:, blk].bitcast(FP8X4), rhs_scale=zs[:, blk], start=True, stop=True)
+
+        def leave(lo, hi, on_scalar):
+            for t in (1, 0, 3, 2):
+                if t in on_scalar:
+                    nc.scalar.activation(out=h2[t][:, lo:hi], in_=h2_ps[t][:, lo:hi], func=ACT.Copy, scale=0.0625)
+                else:
+                    nc.vector.tensor_scalar(out=h2[t][:, lo:hi], in0=h2_ps[t][:, lo:hi], scalar1=0.0625, scalar2=None, op0=ALU.mult)
+
+        fetch_ex(0, BLK, ((0, 0), (1, 0), (2, 0), (3, 0)))
+        (den0,) = add_up((0,))
+        inv0 = invert(den0)
+        fetch_ex(BLK, 3 * BLK, ((2, 1), (3, 0), (3, 1)))
+        den1, den2 = add_up((BLK, 2 * BLK))
+        fetch_ex(3 * BLK, S, ((3, 0), (3, 1)))
+        share(0, inv0)
+        w2w = weight_words("w2", l_k2, "xgw")
+        second(0, w2w)
+        inv1 = invert(den1)
+        (den3,) = add_up((3 * BLK,))
+        share(BLK, inv1)
+        inv2 = invert(den2)
+        second(BLK, w2w)
+        share(2 * BLK, inv2)
+        inv3 = invert(den3)
+        second(2 * BLK, w2w)
+        leave(0, 3 * BLK, (0, 1, 2, 3))
+        share(3 * BLK, inv3)
+        second(3 * BLK, w2w)
+        leave(3 * BLK, S, (0, 2))
+
+        g3 = [held.tile([P, S], F32, name="g3_%d" % t) for t in range(PACK)]
+        st = [held.tile([P, S], F32, name="st%d" % t) for t in range(PACK)]
+        for t in (1, 0, 2, 3):
+            for lo in range(0, S, HALF):
+                gather("v" if t == 1 else "s", g3[t][:, lo : lo + HALF], h2[t], l_n3, lo, lo + HALF)
+            nc.vector.tensor_tensor(out=st[t][:], in0=h2[t][:], in1=g3[t][:], op=ALU.max)
+
+        g4 = held.tile([P, PACK, S], F32, name="g4")
+        res = held.tile([P, PACK, S], F32, name="res")
+        ow = held.tile([P, S], I32, name="ow", align_bytes=64)
+        osc = held.tile([P, S], U8, name="osc", align_bytes=64)
+        out_rows = out_0.rearrange("(p t) j -> p t j", t=PACK)
+        out_words = out_1[0].rearrange("p n t -> p (n t)").bitcast(I32)
+        for lo, hi in ((0, HALF), (HALF, HALF + BLK), (HALF + BLK, S)):
+            for t in (1, 0, 2, 3):
+                gather("v" if (t == 1 and lo == 0) else "s", g4[:, t, lo:hi], st[t], l_n4, lo, hi)
+                nc.vector.tensor_tensor(out=res[:, t, lo:hi], in0=st[t][:, lo:hi], in1=g4[:, t, lo:hi], op=ALU.min)
+            nc.sync.dma_start(out_rows[:, :, lo:hi], res[:, :, lo:hi])
+            ob = held.tile([P, (hi - lo) * PACK], BF16, name="ob%d" % lo, align_bytes=64)
+            nc.vector.tensor_copy(out=ob[:].rearrange("p (c i t) -> p c t i", i=4, t=PACK),
+                                  in_=res[:, :, lo:hi].rearrange("p t (c i) -> p c t i", i=4))
+            nc.vector.quantize_mx(out=ow[:, lo:hi].bitcast(FP8X4), scales=osc[:, lo:hi], in_=ob[:])
+            nc.sync.dma_start(out_words[:, lo:hi], ow[:, lo:hi])
+        out_scales = out_2[0].bitcast(I32)
+        for j in range(4):
+            (nc.sync if j % 2 else nc.scalar).dma_start(out_scales[j:16:4, :], osc[:].bitcast(I32)[j:P:32, :])

@@ -28,8 +28,7 @@ def tile_picked_codesharehopmn_none_po_kernel(tc, x_words, x_scales, d_words, d_
     with ExitStack() as ctx:
         held = ctx.enter_context(tc.tile_pool(name="held", bufs=1))
         ring = ctx.enter_context(tc.tile_pool(name="ring", bufs=2))
-        mm_ps = ctx.enter_context(tc.psum_pool(name="mm_ps", bufs=4))
-        den_ps = ctx.enter_context(tc.psum_pool(name="den_ps", bufs=2))
+        mm_ps = ctx.enter_context(tc.psum_pool(name="mm_ps", bufs=6))
         back_ps = ctx.enter_context(tc.psum_pool(name="back_ps", bufs=2))
 
         def load_list(name, src):
@@ -51,21 +50,17 @@ def tile_picked_codesharehopmn_none_po_kernel(tc, x_words, x_scales, d_words, d_
         ds = held.tile([P, G], U8, name="ds", align_bytes=64)
         xw = held.tile([P, T], I32, name="xw", align_bytes=64)
         xs = held.tile([P, T], U8, name="xs", align_bytes=64)
-        nc.gpsimd.memset(ds[:].bitcast(I32), 0)
-        nc.gpsimd.memset(xs[:].bitcast(I32), 0)
 
         l_k1 = load_list("l_k1", k1)
-        d_rows = d_scales[0].bitcast(I32)
-        for e in range(2):
-            nc.scalar.dma_start(ds[:].bitcast(I32)[e:P:16, :], d_rows[e:16:2, :])
+        nc.sync.dma_start(ds[:].bitcast(I32), d_scales[0].bitcast(I32).unsqueeze(1).broadcast_to([16, 8, G // 4]))
         l_offs = load_list("l_offs", offs)
+        x_rows = x_scales[0].bitcast(I32)
+        for q in range(4):
+            nc.sync.dma_start(xs[:].bitcast(I32)[32 * q : 32 * q + 32, :], x_rows[4 * q : 4 * q + 4, :].unsqueeze(0).broadcast_to([8, 4, T // 4]))
         nc.sync.dma_start(dw[:], d_words[0].rearrange("p n t -> p (n t)").bitcast(I32))
         nc.sync.dma_start(xw[:], x_words[0].rearrange("p n t -> p (n t)").bitcast(I32))
-        x_rows = x_scales[0].bitcast(I32)
-        for j in range(4):
-            nc.scalar.dma_start(xs[:].bitcast(I32)[j:P:32, :], x_rows[j:16:4, :])
         gs_t = held.tile([P, PACK], F32, name="gs_t")
-        nc.sync.dma_start(gs_t[:], gs.rearrange("(p t) o -> p (t o)", t=PACK))
+        nc.gpsimd.dma_start(gs_t[:], gs.rearrange("(p t) o -> p (t o)", t=PACK))
         l_n1 = load_list("l_n1", n1)
         l_n2 = load_list("l_n2", n2)
         l_k2 = load_list("l_k2", k2)
@@ -76,13 +71,13 @@ def tile_picked_codesharehopmn_none_po_kernel(tc, x_words, x_scales, d_words, d_
         make_identity(nc, ident[:])
 
         def weight_scales(tag, lst, queue):
-            got = held.tile([P, S], U8, name=tag + "_sg", align_bytes=64)
+            got = held.tile([P, S], U8, name=tag + "_sg", tag=tag + "_sg", align_bytes=64)
             nc.vector.tensor_copy(out=got[:], in_=ds[:].indirect(lst[:]))
             dealt = held.tile([P, S], U8, name=tag + "_sd", align_bytes=64)
             nc.vector.tensor_copy(out=dealt[:].rearrange("p (t m) -> p m t", t=PACK), in_=got[:].rearrange("p (m t) -> p m t", t=PACK))
             rows = dealt[:].bitcast(I32)
-            for e in range(2):
-                queue.dma_start(rows[2 + e : P : 32, :], rows[16 + e : P : 32, :])
+            for j in range(1, 4):
+                queue.dma_start(rows[j:P:32, :], rows[8 * j : P : 32, :])
             return dealt
 
         def weight_words(tag, lst, slot):
@@ -93,16 +88,15 @@ def tile_picked_codesharehopmn_none_po_kernel(tc, x_words, x_scales, d_words, d_
             return dealt
 
         w1s = weight_scales("w1", l_k1, nc.scalar)
-        w1w = weight_words("w1", l_k1, "w1_wg")
-
         xgw = held.tile([P, S], I32, name="xgw", tag="xgw", align_bytes=64)
-        xgs = held.tile([P, S], U8, name="xgs", align_bytes=64)
+        xgs = held.tile([P, S], U8, name="xgs", tag="w1_sg", align_bytes=64)
         ex = [held.tile([P, S], F32, name="ex%d" % t) for t in range(PACK)]
         exg = held.tile([P, PACK, S], F32, name="exg")
         h_ps = [mm_ps.tile([P, S], F32, name="h_ps", tag="mm") for t in range(PACK)]
+        nc.vector.tensor_copy(out=xgs[:], in_=xs[:].indirect(l_offs[:]))
+        w1w = weight_words("w1", l_k1, "w1_wg")
         for lo in range(0, S, HALF):
             hi = lo + HALF
-            nc.vector.tensor_copy(out=xgs[:, lo:hi], in_=xs[:].indirect(entries(l_offs, lo, hi)))
             nc.vector.tensor_copy(out=xgw[:, lo:hi].bitcast(U32), in_=xw[:].bitcast(U32).indirect(entries(l_offs, lo, hi)))
             for t in range(PACK):
                 cols = slice(t * P, (t + 1) * P)
@@ -113,26 +107,29 @@ def tile_picked_codesharehopmn_none_po_kernel(tc, x_words, x_scales, d_words, d_
             nc.gpsimd.tensor_scalar(out=exg[:, t, :], in0=ex[t][:], scalar1=gs_t[:, t : t + 1], scalar2=0.0, op0=ALU.mult, op1=ALU.add)
 
         w2s = weight_scales("w2", l_k2, nc.sync)
+        w2w = weight_words("w2", l_k2, "xgw")
 
         e1 = [held.tile([P, S], F32, name="e1_%d" % t) for t in range(PACK)]
         e2 = [held.tile([P, S], F32, name="e2_%d" % t) for t in range(PACK)]
         zw = held.tile([P, S], I32, name="zw", align_bytes=64)
         zs = held.tile([P, S], U8, name="zs", align_bytes=64)
-        h2_ps = [mm_ps.tile([P, S], F32, name="h2_ps", tag="mm") for t in range(PACK)]
         h2 = [held.tile([P, S], F32, name="h2_%d" % t) for t in range(PACK)]
 
-        def fetch_ex(lo, hi, on_scalar):
-            for t in range(PACK):
-                for which, (dst, lst) in enumerate(((e1, l_n1), (e2, l_n2))):
-                    gather("s" if (t, which) in on_scalar else "v", dst[t][:, lo:hi], ex[t], lst, lo, hi)
+        fetched = ((e1, l_n1), (e2, l_n2))
 
-        def add_up(blocks):
-            dens = [den_ps.tile([P, PACK, BLK], F32, name="den") for lo in blocks]
+        def open_sum(lo):
+            den = mm_ps.tile([P, PACK, BLK], F32, name="den", tag="mm")
             for t in range(PACK):
-                for den, lo in zip(dens, blocks):
-                    for n, src in enumerate((ex, e1, e2)):
-                        nc.tensor.matmul(den[:, t, :], src[t][:, lo : lo + BLK], ident[:], start=(n == 0), stop=(n == 2), is_transpose=True)
-            return dens
+                nc.tensor.matmul(den[:, t, :], ex[t][:, lo : lo + BLK], ident[:], start=(t == 0), stop=False, is_transpose=True)
+            return den
+
+        def fetch_ex(lo, dens, order):
+            hi = lo + BLK * len(dens)
+            for n, (engine, t, which) in enumerate(order):
+                dst, lst = fetched[which]
+                gather(engine, dst[t][:, lo:hi], ex[t], lst, lo, hi)
+                for b, den in enumerate(dens):
+                    nc.tensor.matmul(den[:, t, :], dst[t][:, lo + b * BLK : lo + (b + 1) * BLK], ident[:], start=False, stop=(n == len(order) - 1), is_transpose=True)
 
         def invert(den):
             root_t = ring.tile([P, PACK, BLK], F32, name="root_t")
@@ -152,47 +149,54 @@ def tile_picked_codesharehopmn_none_po_kernel(tc, x_words, x_scales, d_words, d_
                                     in1=inv[:].rearrange("p t (c i) -> p c t i", i=4), op=ALU.mult)
             nc.vector.quantize_mx(out=zw[:, blk].bitcast(FP8X4), scales=zs[:, blk], in_=zb[:])
 
-        def second(lo, w2w):
-            blk = slice(lo, lo + BLK)
+        def pair_banks(width):
+            return [mm_ps.tile([P, 2, width], F32, name="h2_ps", tag="mm") for u in range(2)]
+
+        def second(lo, banks, at):
             for t in range(PACK):
                 cols = slice(t * P, (t + 1) * P)
-                nc.tensor.matmul_mx(out=h2_ps[t][:, blk], lhsT=w2w[:, cols].bitcast(FP8X4), lhsT_scale=w2s[:, cols],
-                                    rhs=zw[:, blk].bitcast(FP8X4), rhs_scale=zs[:, blk], start=True, stop=True)
+                nc.tensor.matmul_mx(out=banks[t // 2][:, t % 2, at : at + BLK], lhsT=w2w[:, cols].bitcast(FP8X4), lhsT_scale=w2s[:, cols],
+                                    rhs=zw[:, lo : lo + BLK].bitcast(FP8X4), rhs_scale=zs[:, lo : lo + BLK], start=True, stop=True)
 
-        def leave(lo, hi, on_scalar):
-            for t in (1, 0, 3, 2):
+        def leave(lo, hi, banks, on_scalar):
+            for t in range(PACK):
                 if t in on_scalar:
-                    nc.scalar.activation(out=h2[t][:, lo:hi], in_=h2_ps[t][:, lo:hi], func=ACT.Copy, scale=0.0625)
+                    nc.scalar.activation(out=h2[t][:, lo:hi], in_=banks[t // 2][:, t % 2, :], func=ACT.Copy, scale=0.0625)
                 else:
-                    nc.vector.tensor_scalar(out=h2[t][:, lo:hi], in0=h2_ps[t][:, lo:hi], scalar1=0.0625, scalar2=None, op0=ALU.mult)
+                    nc.vector.tensor_scalar(out=h2[t][:, lo:hi], in0=banks[t // 2][:, t % 2, :], scalar1=0.0625, scalar2=None, op0=ALU.mult)
 
-        fetch_ex(0, BLK, ((0, 0), (1, 0), (2, 0), (3, 0)))
-        (den0,) = add_up((0,))
+        den0 = open_sum(0)
+        den1 = open_sum(BLK)
+        den2 = open_sum(2 * BLK)
+        den3 = open_sum(3 * BLK)
+        fetch_ex(0, [den0], (("s", 0, 0), ("v", 0, 1), ("s", 1, 0), ("v", 1, 1), ("s", 2, 0), ("v", 2, 1), ("s", 3, 0), ("v", 3, 1),))
         inv0 = invert(den0)
-        fetch_ex(BLK, 3 * BLK, ((2, 1), (3, 0), (3, 1)))
-        den1, den2 = add_up((BLK, 2 * BLK))
-        fetch_ex(3 * BLK, S, ((3, 0), (3, 1)))
-        share(0, inv0)
-        w2w = weight_words("w2", l_k2, "xgw")
-        second(0, w2w)
+        fetch_ex(BLK, [den1, den2], (("s", 3, 1), ("s", 3, 0), ("v", 0, 0), ("v", 0, 1), ("v", 1, 0), ("v", 1, 1), ("v", 2, 0), ("v", 2, 1),))
         inv1 = invert(den1)
-        (den3,) = add_up((3 * BLK,))
-        share(BLK, inv1)
         inv2 = invert(den2)
-        second(BLK, w2w)
-        share(2 * BLK, inv2)
+        fetch_ex(3 * BLK, [den3], (("s", 3, 1), ("s", 3, 0), ("v", 0, 0), ("v", 0, 1), ("v", 1, 0), ("v", 1, 1), ("v", 2, 0), ("v", 2, 1),))
         inv3 = invert(den3)
-        second(2 * BLK, w2w)
-        leave(0, 3 * BLK, (0, 1, 2, 3))
+        banks01 = pair_banks(HALF)
+        share(0, inv0)
+        second(0, banks01, 0)
+        share(BLK, inv1)
+        second(BLK, banks01, BLK)
+        leave(0, HALF, banks01, (0,1,2,3))
+        share(2 * BLK, inv2)
+        banks2 = pair_banks(BLK)
+        second(2 * BLK, banks2, 0)
+        leave(2 * BLK, 3 * BLK, banks2, (0,1))
         share(3 * BLK, inv3)
-        second(3 * BLK, w2w)
-        leave(3 * BLK, S, (0, 2))
+        banks3 = pair_banks(BLK)
+        second(3 * BLK, banks3, 0)
+        leave(3 * BLK, S, banks3, (0,1))
 
         g3 = [held.tile([P, S], F32, name="g3_%d" % t) for t in range(PACK)]
         st = [held.tile([P, S], F32, name="st%d" % t) for t in range(PACK)]
-        for t in (1, 0, 2, 3):
+        for t in (2, 0, 1, 3):
             for lo in range(0, S, HALF):
-                gather("v" if t == 1 else "s", g3[t][:, lo : lo + HALF], h2[t], l_n3, lo, lo + HALF)
+                gather("v" if (t, lo) in ((2,0),(2,256),(3,0)) else "s", g3[t][:, lo : lo + HALF], h2[t], l_n3, lo, lo + HALF)
+        for t in (2, 0, 1, 3):
             nc.vector.tensor_tensor(out=st[t][:], in0=h2[t][:], in1=g3[t][:], op=ALU.max)
 
         g4 = held.tile([P, PACK, S], F32, name="g4")
@@ -202,8 +206,8 @@ def tile_picked_codesharehopmn_none_po_kernel(tc, x_words, x_scales, d_words, d_
         out_rows = out_0.rearrange("(p t) j -> p t j", t=PACK)
         out_words = out_1[0].rearrange("p n t -> p (n t)").bitcast(I32)
         for lo, hi in ((0, HALF), (HALF, HALF + BLK), (HALF + BLK, S)):
-            for t in (1, 0, 2, 3):
-                gather("v" if (t == 1 and lo == 0) else "s", g4[:, t, lo:hi], st[t], l_n4, lo, hi)
+            for t in (2, 0, 1, 3):
+                gather("v" if (t, lo) in () else "s", g4[:, t, lo:hi], st[t], l_n4, lo, hi)
                 nc.vector.tensor_tensor(out=res[:, t, lo:hi], in0=st[t][:, lo:hi], in1=g4[:, t, lo:hi], op=ALU.min)
             nc.sync.dma_start(out_rows[:, :, lo:hi], res[:, :, lo:hi])
             ob = held.tile([P, (hi - lo) * PACK], BF16, name="ob%d" % lo, align_bytes=64)

@@ -48,7 +48,7 @@ def tile_picked_codesharehopmn_none_po_kernel(tc, x_words, x_scales, d_words, d_
 
         dw = held.tile([P, G], I32, name="dw", align_bytes=64)
         ds = held.tile([P, G], U8, name="ds", align_bytes=64)
-        xw = held.tile([P, T], I32, name="xw", align_bytes=64)
+        xw = held.tile([P, T], I32, name="xw", tag="xw", align_bytes=64)
         xs = held.tile([P, T], U8, name="xs", align_bytes=64)
 
         l_k1 = load_list("l_k1", k1)
@@ -70,8 +70,8 @@ def tile_picked_codesharehopmn_none_po_kernel(tc, x_words, x_scales, d_words, d_
         ident = held.tile([P, P], F32, name="ident")
         make_identity(nc, ident[:])
 
-        def weight_scales(tag, lst, queue):
-            got = held.tile([P, S], U8, name=tag + "_sg", tag=tag + "_sg", align_bytes=64)
+        def weight_scales(tag, lst, queue, slot):
+            got = held.tile([P, S], U8, name=tag + "_sg", tag=slot, align_bytes=64)
             nc.vector.tensor_copy(out=got[:], in_=ds[:].indirect(lst[:]))
             dealt = held.tile([P, S], U8, name=tag + "_sd", align_bytes=64)
             nc.vector.tensor_copy(out=dealt[:].rearrange("p (t m) -> p m t", t=PACK), in_=got[:].rearrange("p (m t) -> p m t", t=PACK))
@@ -87,10 +87,10 @@ def tile_picked_codesharehopmn_none_po_kernel(tc, x_words, x_scales, d_words, d_
             nc.vector.tensor_copy(out=dealt[:].rearrange("p (t m) -> p m t", t=PACK), in_=got[:].rearrange("p (m t) -> p m t", t=PACK))
             return dealt
 
-        w1s = weight_scales("w1", l_k1, nc.scalar)
+        w1s = weight_scales("w1", l_k1, nc.scalar, "w1_sg")
         xgw = held.tile([P, S], I32, name="xgw", tag="xgw", align_bytes=64)
-        xgs = held.tile([P, S], U8, name="xgs", tag="w1_sg", align_bytes=64)
-        ex = [held.tile([P, S], F32, name="ex%d" % t) for t in range(PACK)]
+        xgs = held.tile([P, S], U8, name="xgs", align_bytes=64)
+        ex = [held.tile([P, S], F32, name="ex%d" % t, tag="ex%d" % t, align_bytes=64) for t in range(PACK)]
         exg = held.tile([P, PACK, S], F32, name="exg")
         h_ps = [mm_ps.tile([P, S], F32, name="h_ps", tag="mm") for t in range(PACK)]
         nc.vector.tensor_copy(out=xgs[:], in_=xs[:].indirect(l_offs[:]))
@@ -103,11 +103,8 @@ def tile_picked_codesharehopmn_none_po_kernel(tc, x_words, x_scales, d_words, d_
                 nc.tensor.matmul_mx(out=h_ps[t][:, lo:hi], lhsT=w1w[:, cols].bitcast(FP8X4), lhsT_scale=w1s[:, cols],
                                     rhs=xgw[:, lo:hi].bitcast(FP8X4), rhs_scale=xgs[:, lo:hi], start=True, stop=True)
                 nc.scalar.activation(out=ex[t][:, lo:hi], in_=h_ps[t][:, lo:hi], func=ACT.Exp, scale=0.5 * 0.0625)
-        for t in range(PACK):
-            nc.gpsimd.tensor_scalar(out=exg[:, t, :], in0=ex[t][:], scalar1=gs_t[:, t : t + 1], scalar2=0.0, op0=ALU.mult, op1=ALU.add)
 
-        w2s = weight_scales("w2", l_k2, nc.sync)
-        w2w = weight_words("w2", l_k2, "xgw")
+        w2s = weight_scales("w2", l_k2, nc.sync, "xw")
 
         e1 = [held.tile([P, S], F32, name="e1_%d" % t) for t in range(PACK)]
         e2 = [held.tile([P, S], F32, name="e2_%d" % t) for t in range(PACK)]
@@ -141,22 +138,24 @@ def tile_picked_codesharehopmn_none_po_kernel(tc, x_words, x_scales, d_words, d_
                 nc.tensor.transpose(inv[:, t, :], inv_t[:, t, :], ident[:])
             return inv
 
-        def share(lo, inv):
-            blk = slice(lo, lo + BLK)
-            zb = ring.tile([P, BLK * PACK], BF16, name="zb", align_bytes=64)
-            nc.vector.tensor_tensor(out=zb[:].rearrange("p (c i t) -> p c t i", i=4, t=PACK),
-                                    in0=exg[:, :, blk].rearrange("p t (c i) -> p c t i", i=4),
-                                    in1=inv[:].rearrange("p t (c i) -> p c t i", i=4), op=ALU.mult)
-            nc.vector.quantize_mx(out=zw[:, blk].bitcast(FP8X4), scales=zs[:, blk], in_=zb[:])
+        def share(lo, invs):
+            zb = held.tile([P, len(invs), BLK * PACK], BF16, name="zb%d" % lo, align_bytes=64)
+            for b, inv in enumerate(invs):
+                blk = slice(lo + b * BLK, lo + (b + 1) * BLK)
+                nc.vector.tensor_tensor(out=zb[:, b, :].rearrange("p (c i t) -> p c t i", i=4, t=PACK),
+                                        in0=exg[:, :, blk].rearrange("p t (c i) -> p c t i", i=4),
+                                        in1=inv[:].rearrange("p t (c i) -> p c t i", i=4), op=ALU.mult)
+            cols = slice(lo, lo + BLK * len(invs))
+            nc.vector.quantize_mx(out=zw[:, cols].bitcast(FP8X4), scales=zs[:, cols], in_=zb[:].rearrange("p b c -> p (b c)"))
 
         def pair_banks(width):
             return [mm_ps.tile([P, 2, width], F32, name="h2_ps", tag="mm") for u in range(2)]
 
-        def second(lo, banks, at):
+        def second(lo, hi, banks):
             for t in range(PACK):
                 cols = slice(t * P, (t + 1) * P)
-                nc.tensor.matmul_mx(out=banks[t // 2][:, t % 2, at : at + BLK], lhsT=w2w[:, cols].bitcast(FP8X4), lhsT_scale=w2s[:, cols],
-                                    rhs=zw[:, lo : lo + BLK].bitcast(FP8X4), rhs_scale=zs[:, lo : lo + BLK], start=True, stop=True)
+                nc.tensor.matmul_mx(out=banks[t // 2][:, t % 2, :], lhsT=w2w[:, cols].bitcast(FP8X4), lhsT_scale=w2s[:, cols],
+                                    rhs=zw[:, lo:hi].bitcast(FP8X4), rhs_scale=zs[:, lo:hi], start=True, stop=True)
 
         def leave(lo, hi, banks, on_scalar):
             for t in range(PACK):
@@ -174,24 +173,25 @@ def tile_picked_codesharehopmn_none_po_kernel(tc, x_words, x_scales, d_words, d_
         fetch_ex(BLK, [den1, den2], (("s", 3, 1), ("s", 3, 0), ("v", 0, 0), ("v", 0, 1), ("v", 1, 0), ("v", 1, 1), ("v", 2, 0), ("v", 2, 1),))
         inv1 = invert(den1)
         inv2 = invert(den2)
-        fetch_ex(3 * BLK, [den3], (("s", 3, 1), ("s", 3, 0), ("v", 0, 0), ("v", 0, 1), ("v", 1, 0), ("v", 1, 1), ("v", 2, 0), ("v", 2, 1),))
+        fetch_ex(3 * BLK, [den3], (("s", 3, 1), ("s", 3, 0), ("s", 2, 1), ("v", 0, 0), ("v", 0, 1), ("v", 1, 0), ("v", 1, 1), ("v", 2, 0),))
         inv3 = invert(den3)
+        for t in range(PACK):
+            nc.vector.tensor_scalar(out=exg[:, t, :], in0=ex[t][:], scalar1=gs_t[:, t : t + 1], scalar2=None, op0=ALU.mult)
+        w2w = weight_words("w2", l_k2, "ex2")
         banks01 = pair_banks(HALF)
-        share(0, inv0)
-        second(0, banks01, 0)
-        share(BLK, inv1)
-        second(BLK, banks01, BLK)
+        share(0, [inv0, inv1])
+        second(0, HALF, banks01)
         leave(0, HALF, banks01, (0,1,2,3))
-        share(2 * BLK, inv2)
+        share(2 * BLK, [inv2])
         banks2 = pair_banks(BLK)
-        second(2 * BLK, banks2, 0)
+        second(2 * BLK, 3 * BLK, banks2)
         leave(2 * BLK, 3 * BLK, banks2, (0,1))
-        share(3 * BLK, inv3)
+        share(3 * BLK, [inv3])
         banks3 = pair_banks(BLK)
-        second(3 * BLK, banks3, 0)
+        second(3 * BLK, S, banks3)
         leave(3 * BLK, S, banks3, (0,1))
 
-        g3 = [held.tile([P, S], F32, name="g3_%d" % t) for t in range(PACK)]
+        g3 = [held.tile([P, S], F32, name="g3_%d" % t, tag="g3_%d" % t) for t in range(PACK)]
         st = [held.tile([P, S], F32, name="st%d" % t) for t in range(PACK)]
         for t in (2, 0, 1, 3):
             for lo in range(0, S, HALF):
@@ -199,16 +199,16 @@ def tile_picked_codesharehopmn_none_po_kernel(tc, x_words, x_scales, d_words, d_
         for t in (2, 0, 1, 3):
             nc.vector.tensor_tensor(out=st[t][:], in0=h2[t][:], in1=g3[t][:], op=ALU.max)
 
-        g4 = held.tile([P, PACK, S], F32, name="g4")
         res = held.tile([P, PACK, S], F32, name="res")
         ow = held.tile([P, S], I32, name="ow", align_bytes=64)
         osc = held.tile([P, S], U8, name="osc", align_bytes=64)
         out_rows = out_0.rearrange("(p t) j -> p t j", t=PACK)
         out_words = out_1[0].rearrange("p n t -> p (n t)").bitcast(I32)
         for lo, hi in ((0, HALF), (HALF, HALF + BLK), (HALF + BLK, S)):
+            g4 = held.tile([P, PACK, hi - lo], F32, name="g4", tag="g3_3" if lo == HALF else "g4")
             for t in (2, 0, 1, 3):
-                gather("v" if (t, lo) in () else "s", g4[:, t, lo:hi], st[t], l_n4, lo, hi)
-                nc.vector.tensor_tensor(out=res[:, t, lo:hi], in0=st[t][:, lo:hi], in1=g4[:, t, lo:hi], op=ALU.min)
+                gather("v" if (t, lo) in () else "s", g4[:, t, :], st[t], l_n4, lo, hi)
+                nc.vector.tensor_tensor(out=res[:, t, lo:hi], in0=st[t][:, lo:hi], in1=g4[:, t, :], op=ALU.min)
             nc.sync.dma_start(out_rows[:, :, lo:hi], res[:, :, lo:hi])
             ob = held.tile([P, (hi - lo) * PACK], BF16, name="ob%d" % lo, align_bytes=64)
             nc.vector.tensor_copy(out=ob[:].rearrange("p (c i t) -> p c t i", i=4, t=PACK),

@@ -18,33 +18,46 @@ PACK = 4
 S = 512
 T = 1024
 G = 2048
-HALF = 256
+SCALE_ROWS = 16
+QUADRANT = 32
+GROUP = 16
+HALF = S // 2
 BLK = 128
+LINE = 4
+SIXTEENTH = 0.0625
 FLOPS = 2 * 2 * 512 * 512 * 512
 
 
-def tile_picked_codesharehopmn_none_po_kernel(tc, x_words, x_scales, d_words, d_scales, gs, offs, k1, n1, n2, k2, n3, n4, out_0, out_1, out_2):
+def tile_picked_codesharehopmn_none_po_kernel(
+    tc, x_words, x_scales, d_words, d_scales, gs, offs, k1, n1, n2, k2, n3, n4, out_0, out_1, out_2
+):
     nc = tc.nc
     with ExitStack() as ctx:
         held = ctx.enter_context(tc.tile_pool(name="held", bufs=1))
         ring = ctx.enter_context(tc.tile_pool(name="ring", bufs=2))
-        mm_ps = ctx.enter_context(tc.psum_pool(name="mm_ps", bufs=6))
+        mm_ps = ctx.enter_context(tc.psum_pool(name="mm_ps", bufs=PACK))
         back_ps = ctx.enter_context(tc.psum_pool(name="back_ps", bufs=2))
 
         def load_list(name, src):
-            tile = held.tile([P, S // 16], U16, name=name)
+            tile = held.tile([P, S // GROUP], U16, name=name)
             nc.sync.dma_start(tile[:], src)
             return tile
 
         def entries(lst, lo, hi):
-            return lst[:, lo // 16 : hi // 16]
+            return lst[:, lo // GROUP : hi // GROUP]
 
-        def gather(engine, out, window, lst, lo, hi):
+        def gather(on_scalar, out, window, lst, lo, hi):
             src = window[:].indirect(entries(lst, lo, hi))
-            if engine == "s":
+            if on_scalar:
                 nc.scalar.activation(out=out, in_=src, func=ACT.Copy)
             else:
                 nc.vector.tensor_copy(out=out, in_=src)
+
+        def interleaved(flat):
+            return flat.rearrange("p (c i t) -> p c t i", i=LINE, t=PACK)
+
+        def by_runs(tiles):
+            return tiles.rearrange("p t (c i) -> p c t i", i=LINE)
 
         dw = held.tile([P, G], I32, name="dw", align_bytes=64)
         ds = held.tile([P, G], U8, name="ds", align_bytes=64)
@@ -52,11 +65,17 @@ def tile_picked_codesharehopmn_none_po_kernel(tc, x_words, x_scales, d_words, d_
         xs = held.tile([P, T], U8, name="xs", align_bytes=64)
 
         l_k1 = load_list("l_k1", k1)
-        nc.sync.dma_start(ds[:].bitcast(I32), d_scales[0].bitcast(I32).unsqueeze(1).broadcast_to([16, 8, G // 4]))
+        nc.sync.dma_start(
+            ds[:].bitcast(I32),
+            d_scales[0].bitcast(I32).unsqueeze(1).broadcast_to([SCALE_ROWS, P // SCALE_ROWS, G // 4]),
+        )
         l_offs = load_list("l_offs", offs)
         x_rows = x_scales[0].bitcast(I32)
-        for q in range(4):
-            nc.sync.dma_start(xs[:].bitcast(I32)[32 * q : 32 * q + 32, :], x_rows[4 * q : 4 * q + 4, :].unsqueeze(0).broadcast_to([8, 4, T // 4]))
+        for q in range(P // QUADRANT):
+            nc.sync.dma_start(
+                xs[:].bitcast(I32)[QUADRANT * q : QUADRANT * (q + 1), :],
+                x_rows[4 * q : 4 * (q + 1), :].unsqueeze(0).broadcast_to([QUADRANT // 4, 4, T // 4]),
+            )
         nc.sync.dma_start(dw[:], d_words[0].rearrange("p n t -> p (n t)").bitcast(I32))
         nc.sync.dma_start(xw[:], x_words[0].rearrange("p n t -> p (n t)").bitcast(I32))
         gs_t = held.tile([P, PACK], F32, name="gs_t")
@@ -70,67 +89,97 @@ def tile_picked_codesharehopmn_none_po_kernel(tc, x_words, x_scales, d_words, d_
         ident = held.tile([P, P], F32, name="ident")
         make_identity(nc, ident[:])
 
-        def weight_scales(tag, lst, queue, slot):
-            got = held.tile([P, S], U8, name=tag + "_sg", tag=slot, align_bytes=64)
-            nc.vector.tensor_copy(out=got[:], in_=ds[:].indirect(lst[:]))
-            dealt = held.tile([P, S], U8, name=tag + "_sd", align_bytes=64)
-            nc.vector.tensor_copy(out=dealt[:].rearrange("p (t m) -> p m t", t=PACK), in_=got[:].rearrange("p (m t) -> p m t", t=PACK))
+        def deal(dealt, picked):
+            nc.vector.tensor_copy(
+                out=dealt[:].rearrange("p (t m) -> p m t", t=PACK),
+                in_=picked[:].rearrange("p (m t) -> p m t", t=PACK),
+            )
+
+        def weight_scales(name, lst, queue, slot):
+            picked = held.tile([P, S], U8, name=name + "_picked_scales", tag=slot, align_bytes=64)
+            nc.vector.tensor_copy(out=picked[:], in_=ds[:].indirect(lst[:]))
+            dealt = held.tile([P, S], U8, name=name + "_scales", align_bytes=64)
+            deal(dealt, picked)
             rows = dealt[:].bitcast(I32)
             for j in range(1, 4):
-                queue.dma_start(rows[j:P:32, :], rows[8 * j : P : 32, :])
+                queue.dma_start(rows[j:P:QUADRANT, :], rows[8 * j : P : QUADRANT, :])
             return dealt
 
-        def weight_words(tag, lst, slot):
-            got = held.tile([P, S], I32, name=tag + "_wg", tag=slot, align_bytes=64)
-            nc.vector.tensor_copy(out=got[:].bitcast(U32), in_=dw[:].bitcast(U32).indirect(lst[:]))
-            dealt = held.tile([P, S], I32, name=tag + "_wd", align_bytes=64)
-            nc.vector.tensor_copy(out=dealt[:].rearrange("p (t m) -> p m t", t=PACK), in_=got[:].rearrange("p (m t) -> p m t", t=PACK))
+        def weight_words(name, lst, slot):
+            picked = held.tile([P, S], I32, name=name + "_picked_words", tag=slot, align_bytes=64)
+            nc.vector.tensor_copy(out=picked[:].bitcast(U32), in_=dw[:].bitcast(U32).indirect(lst[:]))
+            dealt = held.tile([P, S], I32, name=name + "_words", align_bytes=64)
+            deal(dealt, picked)
             return dealt
 
-        w1s = weight_scales("w1", l_k1, nc.scalar, "w1_sg")
-        xgw = held.tile([P, S], I32, name="xgw", tag="xgw", align_bytes=64)
+        def product(out, words, scales, t, rhs_words, rhs_scales):
+            cols = slice(t * P, (t + 1) * P)
+            nc.tensor.matmul_mx(
+                out=out,
+                lhsT=words[:, cols].bitcast(FP8X4),
+                lhsT_scale=scales[:, cols],
+                rhs=rhs_words.bitcast(FP8X4),
+                rhs_scale=rhs_scales,
+                start=True,
+                stop=True,
+            )
+
+        w1s = weight_scales("w1", l_k1, nc.scalar, "w1_picked_scales")
+        xgw = held.tile([P, S], I32, name="xgw", align_bytes=64)
         xgs = held.tile([P, S], U8, name="xgs", align_bytes=64)
         ex = [held.tile([P, S], F32, name="ex%d" % t, tag="ex%d" % t, align_bytes=64) for t in range(PACK)]
-        exg = held.tile([P, PACK, S], F32, name="exg")
-        h_ps = [mm_ps.tile([P, S], F32, name="h_ps", tag="mm") for t in range(PACK)]
+        h_ps = [mm_ps.tile([P, S], F32, name="h_ps", tag="turn") for t in range(PACK)]
         nc.vector.tensor_copy(out=xgs[:], in_=xs[:].indirect(l_offs[:]))
-        w1w = weight_words("w1", l_k1, "w1_wg")
+        w1w = weight_words("w1", l_k1, "w1_picked_words")
         for lo in range(0, S, HALF):
             hi = lo + HALF
-            nc.vector.tensor_copy(out=xgw[:, lo:hi].bitcast(U32), in_=xw[:].bitcast(U32).indirect(entries(l_offs, lo, hi)))
+            nc.vector.tensor_copy(
+                out=xgw[:, lo:hi].bitcast(U32), in_=xw[:].bitcast(U32).indirect(entries(l_offs, lo, hi))
+            )
             for t in range(PACK):
-                cols = slice(t * P, (t + 1) * P)
-                nc.tensor.matmul_mx(out=h_ps[t][:, lo:hi], lhsT=w1w[:, cols].bitcast(FP8X4), lhsT_scale=w1s[:, cols],
-                                    rhs=xgw[:, lo:hi].bitcast(FP8X4), rhs_scale=xgs[:, lo:hi], start=True, stop=True)
-                nc.scalar.activation(out=ex[t][:, lo:hi], in_=h_ps[t][:, lo:hi], func=ACT.Exp, scale=0.5 * 0.0625)
+                product(h_ps[t][:, lo:hi], w1w, w1s, t, xgw[:, lo:hi], xgs[:, lo:hi])
+                nc.scalar.activation(out=ex[t][:, lo:hi], in_=h_ps[t][:, lo:hi], func=ACT.Exp, scale=0.5 * SIXTEENTH)
 
         w2s = weight_scales("w2", l_k2, nc.sync, "xw")
 
         e1 = [held.tile([P, S], F32, name="e1_%d" % t) for t in range(PACK)]
         e2 = [held.tile([P, S], F32, name="e2_%d" % t) for t in range(PACK)]
+        looked_up = ((e1, l_n1), (e2, l_n2))
+        exg = held.tile([P, PACK, S], F32, name="exg")
         zw = held.tile([P, S], I32, name="zw", align_bytes=64)
         zs = held.tile([P, S], U8, name="zs", align_bytes=64)
         h2 = [held.tile([P, S], F32, name="h2_%d" % t) for t in range(PACK)]
 
-        fetched = ((e1, l_n1), (e2, l_n2))
-
         def open_sum(lo):
-            den = mm_ps.tile([P, PACK, BLK], F32, name="den", tag="mm")
+            total = mm_ps.tile([P, PACK, BLK], F32, name="total", tag="turn")
             for t in range(PACK):
-                nc.tensor.matmul(den[:, t, :], ex[t][:, lo : lo + BLK], ident[:], start=(t == 0), stop=False, is_transpose=True)
-            return den
+                nc.tensor.matmul(
+                    total[:, t, :], ex[t][:, lo : lo + BLK], ident[:], start=(t == 0), stop=False, is_transpose=True
+                )
+            return total
 
-        def fetch_ex(lo, dens, order):
-            hi = lo + BLK * len(dens)
-            for n, (engine, t, which) in enumerate(order):
-                dst, lst = fetched[which]
-                gather(engine, dst[t][:, lo:hi], ex[t], lst, lo, hi)
-                for b, den in enumerate(dens):
-                    nc.tensor.matmul(den[:, t, :], dst[t][:, lo + b * BLK : lo + (b + 1) * BLK], ident[:], start=False, stop=(n == len(order) - 1), is_transpose=True)
+        def add_neighbours(lo, totals, order):
+            hi = lo + BLK * len(totals)
+            for step, (on_scalar, t, which) in enumerate(order):
+                terms, lst = looked_up[which]
+                gather(on_scalar, terms[t][:, lo:hi], ex[t], lst, lo, hi)
+                for b, total in enumerate(totals):
+                    nc.tensor.matmul(
+                        total[:, t, :],
+                        terms[t][:, lo + b * BLK : lo + (b + 1) * BLK],
+                        ident[:],
+                        start=False,
+                        stop=(step == len(order) - 1),
+                        is_transpose=True,
+                    )
 
-        def invert(den):
+        def split_by_tile(n_scalar):
+            tiles = list(reversed(range(PACK - n_scalar, PACK))) + list(range(PACK - n_scalar))
+            return [(t >= PACK - n_scalar, t, which) for t in tiles for which in range(2)]
+
+        def invert(total):
             root_t = ring.tile([P, PACK, BLK], F32, name="root_t")
-            nc.scalar.activation(out=root_t[:], in_=den[:], func=ACT.Abs_reciprocal_sqrt, scale=0.5)
+            nc.scalar.activation(out=root_t[:], in_=total[:], func=ACT.Abs_reciprocal_sqrt, scale=0.5)
             inv_t = ring.tile([P, PACK, BLK], F32, name="inv_t")
             nc.scalar.activation(out=inv_t[:], in_=root_t[:], func=ACT.Square)
             inv = back_ps.tile([P, PACK, BLK], F32, name="inv")
@@ -138,65 +187,57 @@ def tile_picked_codesharehopmn_none_po_kernel(tc, x_words, x_scales, d_words, d_
                 nc.tensor.transpose(inv[:, t, :], inv_t[:, t, :], ident[:])
             return inv
 
-        def share(lo, invs):
+        def quantise_z(lo, invs):
             zb = held.tile([P, len(invs), BLK * PACK], BF16, name="zb%d" % lo, align_bytes=64)
             for b, inv in enumerate(invs):
                 blk = slice(lo + b * BLK, lo + (b + 1) * BLK)
-                nc.vector.tensor_tensor(out=zb[:, b, :].rearrange("p (c i t) -> p c t i", i=4, t=PACK),
-                                        in0=exg[:, :, blk].rearrange("p t (c i) -> p c t i", i=4),
-                                        in1=inv[:].rearrange("p t (c i) -> p c t i", i=4), op=ALU.mult)
+                nc.vector.tensor_tensor(
+                    out=interleaved(zb[:, b, :]), in0=by_runs(exg[:, :, blk]), in1=by_runs(inv[:]), op=ALU.mult
+                )
             cols = slice(lo, lo + BLK * len(invs))
-            nc.vector.quantize_mx(out=zw[:, cols].bitcast(FP8X4), scales=zs[:, cols], in_=zb[:].rearrange("p b c -> p (b c)"))
+            nc.vector.quantize_mx(
+                out=zw[:, cols].bitcast(FP8X4), scales=zs[:, cols], in_=zb[:].rearrange("p b c -> p (b c)")
+            )
 
-        def pair_banks(width):
-            return [mm_ps.tile([P, 2, width], F32, name="h2_ps", tag="mm") for u in range(2)]
-
-        def second(lo, hi, banks):
+        def second_layer(lo, hi, tag, bufs, n_scalar):
+            banks = [mm_ps.tile([P, 2, hi - lo], F32, name="h2_ps", tag=tag, bufs=bufs) for pair in range(2)]
             for t in range(PACK):
-                cols = slice(t * P, (t + 1) * P)
-                nc.tensor.matmul_mx(out=banks[t // 2][:, t % 2, :], lhsT=w2w[:, cols].bitcast(FP8X4), lhsT_scale=w2s[:, cols],
-                                    rhs=zw[:, lo:hi].bitcast(FP8X4), rhs_scale=zs[:, lo:hi], start=True, stop=True)
-
-        def leave(lo, hi, banks, on_scalar):
+                product(banks[t // 2][:, t % 2, :], w2w, w2s, t, zw[:, lo:hi], zs[:, lo:hi])
             for t in range(PACK):
-                if t in on_scalar:
-                    nc.scalar.activation(out=h2[t][:, lo:hi], in_=banks[t // 2][:, t % 2, :], func=ACT.Copy, scale=0.0625)
+                sums = banks[t // 2][:, t % 2, :]
+                if t < n_scalar:
+                    nc.scalar.activation(out=h2[t][:, lo:hi], in_=sums, func=ACT.Copy, scale=SIXTEENTH)
                 else:
-                    nc.vector.tensor_scalar(out=h2[t][:, lo:hi], in0=banks[t // 2][:, t % 2, :], scalar1=0.0625, scalar2=None, op0=ALU.mult)
+                    nc.vector.tensor_scalar(out=h2[t][:, lo:hi], in0=sums, scalar1=SIXTEENTH, scalar2=None, op0=ALU.mult)
 
-        den0 = open_sum(0)
-        den1 = open_sum(BLK)
-        den2 = open_sum(2 * BLK)
-        den3 = open_sum(3 * BLK)
-        fetch_ex(0, [den0], (("s", 0, 0), ("v", 0, 1), ("s", 1, 0), ("v", 1, 1), ("s", 2, 0), ("v", 2, 1), ("s", 3, 0), ("v", 3, 1),))
-        inv0 = invert(den0)
-        fetch_ex(BLK, [den1, den2], (("s", 3, 1), ("s", 3, 0), ("v", 0, 0), ("v", 0, 1), ("v", 1, 0), ("v", 1, 1), ("v", 2, 0), ("v", 2, 1),))
-        inv1 = invert(den1)
-        inv2 = invert(den2)
-        fetch_ex(3 * BLK, [den3], (("s", 3, 1), ("s", 3, 0), ("s", 2, 1), ("v", 0, 0), ("v", 0, 1), ("v", 1, 0), ("v", 1, 1), ("v", 2, 0),))
-        inv3 = invert(den3)
+        totals = [open_sum(lo) for lo in range(0, S, BLK)]
+        add_neighbours(0, totals[0:1], [(which == 0, t, which) for t in range(PACK) for which in range(2)])
+        inv0 = invert(totals[0])
+        add_neighbours(BLK, totals[1:3], split_by_tile(1))
+        inv1 = invert(totals[1])
+        inv2 = invert(totals[2])
+        add_neighbours(3 * BLK, totals[3:4], split_by_tile(2))
+        inv3 = invert(totals[3])
         for t in range(PACK):
-            nc.vector.tensor_scalar(out=exg[:, t, :], in0=ex[t][:], scalar1=gs_t[:, t : t + 1], scalar2=None, op0=ALU.mult)
+            nc.vector.tensor_scalar(
+                out=exg[:, t, :], in0=ex[t][:], scalar1=gs_t[:, t : t + 1], scalar2=None, op0=ALU.mult
+            )
         w2w = weight_words("w2", l_k2, "ex2")
-        banks01 = pair_banks(HALF)
-        share(0, [inv0, inv1])
-        second(0, HALF, banks01)
-        leave(0, HALF, banks01, (0,1,2,3))
-        share(2 * BLK, [inv2])
-        banks2 = pair_banks(BLK)
-        second(2 * BLK, 3 * BLK, banks2)
-        leave(2 * BLK, 3 * BLK, banks2, (0,1))
-        share(3 * BLK, [inv3])
-        banks3 = pair_banks(BLK)
-        second(3 * BLK, S, banks3)
-        leave(3 * BLK, S, banks3, (0,1))
+        quantise_z(0, [inv0, inv1])
+        second_layer(0, HALF, "first", 2, PACK)
+        quantise_z(2 * BLK, [inv2])
+        second_layer(2 * BLK, 3 * BLK, "turn", PACK, 2)
+        quantise_z(3 * BLK, [inv3])
+        second_layer(3 * BLK, S, "turn", PACK, 2)
 
+        tile_order = (2, 0, 1, 3)
         g3 = [held.tile([P, S], F32, name="g3_%d" % t, tag="g3_%d" % t) for t in range(PACK)]
         st = [held.tile([P, S], F32, name="st%d" % t) for t in range(PACK)]
-        for t in (2, 0, 1, 3):
+        for t in tile_order:
             for lo in range(0, S, HALF):
-                gather("v" if (t, lo) in ((2,0),(2,256),(3,0)) else "s", g3[t][:, lo : lo + HALF], h2[t], l_n3, lo, lo + HALF)
-        for t in (2, 0, 1, 3):
+                on_vector = t == 2 or (t == 3 and lo == 0)
+                gather(not on_vector, g3[t][:, lo : lo + HALF], h2[t], l_n3, lo, lo + HALF)
+        for t in tile_order:
             nc.vector.tensor_tensor(out=st[t][:], in0=h2[t][:], in1=g3[t][:], op=ALU.max)
 
         res = held.tile([P, PACK, S], F32, name="res")
@@ -204,17 +245,17 @@ def tile_picked_codesharehopmn_none_po_kernel(tc, x_words, x_scales, d_words, d_
         osc = held.tile([P, S], U8, name="osc", align_bytes=64)
         out_rows = out_0.rearrange("(p t) j -> p t j", t=PACK)
         out_words = out_1[0].rearrange("p n t -> p (n t)").bitcast(I32)
-        for lo, hi in ((0, HALF), (HALF, HALF + BLK), (HALF + BLK, S)):
-            g4 = held.tile([P, PACK, hi - lo], F32, name="g4", tag="g3_3" if lo == HALF else "g4")
-            for t in (2, 0, 1, 3):
-                gather("v" if (t, lo) in () else "s", g4[:, t, :], st[t], l_n4, lo, hi)
+        for lo, hi, slot in ((0, HALF, "g4"), (HALF, HALF + BLK, "g3_3"), (HALF + BLK, S, "g4")):
+            g4 = held.tile([P, PACK, hi - lo], F32, name="g4", tag=slot)
+            for t in tile_order:
+                gather(True, g4[:, t, :], st[t], l_n4, lo, hi)
                 nc.vector.tensor_tensor(out=res[:, t, lo:hi], in0=st[t][:, lo:hi], in1=g4[:, t, :], op=ALU.min)
             nc.sync.dma_start(out_rows[:, :, lo:hi], res[:, :, lo:hi])
             ob = held.tile([P, (hi - lo) * PACK], BF16, name="ob%d" % lo, align_bytes=64)
-            nc.vector.tensor_copy(out=ob[:].rearrange("p (c i t) -> p c t i", i=4, t=PACK),
-                                  in_=res[:, :, lo:hi].rearrange("p t (c i) -> p c t i", i=4))
+            nc.vector.tensor_copy(out=interleaved(ob[:]), in_=by_runs(res[:, :, lo:hi]))
             nc.vector.quantize_mx(out=ow[:, lo:hi].bitcast(FP8X4), scales=osc[:, lo:hi], in_=ob[:])
             nc.sync.dma_start(out_words[:, lo:hi], ow[:, lo:hi])
         out_scales = out_2[0].bitcast(I32)
         for j in range(4):
-            (nc.sync if j % 2 else nc.scalar).dma_start(out_scales[j:16:4, :], osc[:].bitcast(I32)[j:P:32, :])
+            queue = nc.sync if j % 2 else nc.scalar
+            queue.dma_start(out_scales[j:SCALE_ROWS:4, :], osc[:].bitcast(I32)[j:P:QUADRANT, :])

from contextlib import ExitStack

import concourse.mybir as mybir
from concourse.masks import make_identity

F32 = mybir.dt.float32
BF16 = mybir.dt.bfloat16
I32 = mybir.dt.int32
U32 = mybir.dt.uint32
U16 = mybir.dt.uint16
U8 = mybir.dt.uint8
FP8X4 = mybir.dt.float8_e4m3fn_x4
ACT = mybir.ActivationFunctionType
ALU = mybir.AluOpType

P = 128
PACK = 4
S = 512
T = 1024
G = 2048
SCALE_ROWS = 16
QUADRANT = 32
GROUP = 16
HALF = S // 2
BLK = 128
LINE = 4
SIXTEENTH = 0.0625
FLOPS = 2 * 2 * 512 * 512 * 512


def tile_picked_codesharehopmn_none_po_kernel(
    tc, x_words, x_scales, d_words, d_scales, gs, offs, k1, n1, n2, k2, n3, n4, out_0, out_1, out_2
):
    nc = tc.nc
    with ExitStack() as ctx:
        held = ctx.enter_context(tc.tile_pool(name="held", bufs=1))
        ring = ctx.enter_context(tc.tile_pool(name="ring", bufs=2))
        mm_ps = ctx.enter_context(tc.psum_pool(name="mm_ps", bufs=PACK))
        back_ps = ctx.enter_context(tc.psum_pool(name="back_ps", bufs=2))

        def load_list(name, src):
            tile = held.tile([P, S // GROUP], U16, name=name)
            nc.sync.dma_start(tile[:], src)
            return tile

        def entries(lst, lo, hi):
            return lst[:, lo // GROUP : hi // GROUP]

        def gather(on_scalar, out, window, lst, lo, hi):
            src = window[:].indirect(entries(lst, lo, hi))
            if on_scalar:
                nc.scalar.activation(out=out, in_=src, func=ACT.Copy)
            else:
                nc.vector.tensor_copy(out=out, in_=src)

        def interleaved(flat):
            return flat.rearrange("p (c i t) -> p c t i", i=LINE, t=PACK)

        def by_runs(tiles):
            return tiles.rearrange("p t (c i) -> p c t i", i=LINE)

        dw = held.tile([P, G], I32, name="dw", align_bytes=64)
        ds = held.tile([P, G], U8, name="ds", align_bytes=64)
        xw = held.tile([P, T], I32, name="xw", tag="xw", align_bytes=64)
        xs = held.tile([P, T], U8, name="xs", align_bytes=64)

        l_k1 = load_list("l_k1", k1)
        nc.sync.dma_start(
            ds[:].bitcast(I32),
            d_scales[0].bitcast(I32).unsqueeze(1).broadcast_to([SCALE_ROWS, P // SCALE_ROWS, G // 4]),
        )
        l_offs = load_list("l_offs", offs)
        x_rows = x_scales[0].bitcast(I32)
        for q in range(P // QUADRANT):
            nc.sync.dma_start(
                xs[:].bitcast(I32)[QUADRANT * q : QUADRANT * (q + 1), :],
                x_rows[4 * q : 4 * (q + 1), :].unsqueeze(0).broadcast_to([QUADRANT // 4, 4, T // 4]),
            )
        nc.sync.dma_start(dw[:], d_words[0].rearrange("p n t -> p (n t)").bitcast(I32))
        nc.sync.dma_start(xw[:], x_words[0].rearrange("p n t -> p (n t)").bitcast(I32))
        gs_t = held.tile([P, PACK], F32, name="gs_t")
        nc.gpsimd.dma_start(gs_t[:], gs.rearrange("(p t) o -> p (t o)", t=PACK))
        l_n1 = load_list("l_n1", n1)
        l_n2 = load_list("l_n2", n2)
        l_k2 = load_list("l_k2", k2)
        l_n3 = load_list("l_n3", n3)
        l_n4 = load_list("l_n4", n4)

        ident = held.tile([P, P], F32, name="ident")
        make_identity(nc, ident[:])

        def deal(dealt, picked):
            nc.vector.tensor_copy(
                out=dealt[:].rearrange("p (t m) -> p m t", t=PACK),
                in_=picked[:].rearrange("p (m t) -> p m t", t=PACK),
            )

        def weight_scales(name, lst, queue, slot):
            picked = held.tile([P, S], U8, name=name + "_picked_scales", tag=slot, align_bytes=64)
            nc.vector.tensor_copy(out=picked[:], in_=ds[:].indirect(lst[:]))
            dealt = held.tile([P, S], U8, name=name + "_scales", align_bytes=64)
            deal(dealt, picked)
            rows = dealt[:].bitcast(I32)
            for j in range(1, 4):
                queue.dma_start(rows[j:P:QUADRANT, :], rows[8 * j : P : QUADRANT, :])
            return dealt

        def weight_words(name, lst, slot):
            picked = held.tile([P, S], I32, name=name + "_picked_words", tag=slot, align_bytes=64)
            nc.vector.tensor_copy(out=picked[:].bitcast(U32), in_=dw[:].bitcast(U32).indirect(lst[:]))
            dealt = held.tile([P, S], I32, name=name + "_words", align_bytes=64)
            deal(dealt, picked)
            return dealt

        def product(out, words, scales, t, rhs_words, rhs_scales):
            cols = slice(t * P, (t + 1) * P)
            nc.tensor.matmul_mx(
                out=out,
                lhsT=words[:, cols].bitcast(FP8X4),
                lhsT_scale=scales[:, cols],
                rhs=rhs_words.bitcast(FP8X4),
                rhs_scale=rhs_scales,
                start=True,
                stop=True,
            )

        w1s = weight_scales("w1", l_k1, nc.scalar, "w1_picked_scales")
        xgw = held.tile([P, S], I32, name="xgw", align_bytes=64)
        xgs = held.tile([P, S], U8, name="xgs", align_bytes=64)
        ex = [held.tile([P, S], F32, name="ex%d" % t, tag="ex%d" % t, align_bytes=64) for t in range(PACK)]
        h_ps = [mm_ps.tile([P, S], F32, name="h_ps", tag="turn") for t in range(PACK)]
        nc.vector.tensor_copy(out=xgs[:], in_=xs[:].indirect(l_offs[:]))
        w1w = weight_words("w1", l_k1, "w1_picked_words")
        for lo in range(0, S, HALF):
            hi = lo + HALF
            nc.vector.tensor_copy(
                out=xgw[:, lo:hi].bitcast(U32), in_=xw[:].bitcast(U32).indirect(entries(l_offs, lo, hi))
            )
            for t in range(PACK):
                product(h_ps[t][:, lo:hi], w1w, w1s, t, xgw[:, lo:hi], xgs[:, lo:hi])
                nc.scalar.activation(out=ex[t][:, lo:hi], in_=h_ps[t][:, lo:hi], func=ACT.Exp, scale=0.5 * SIXTEENTH)

        w2s = weight_scales("w2", l_k2, nc.sync, "xw")

        e1 = [held.tile([P, S], F32, name="e1_%d" % t) for t in range(PACK)]
        e2 = [held.tile([P, S], F32, name="e2_%d" % t) for t in range(PACK)]
        looked_up = ((e1, l_n1), (e2, l_n2))
        exg = held.tile([P, PACK, S], F32, name="exg")
        zw = held.tile([P, S], I32, name="zw", align_bytes=64)
        zs = held.tile([P, S], U8, name="zs", align_bytes=64)
        h2 = [held.tile([P, S], F32, name="h2_%d" % t) for t in range(PACK)]

        def open_sum(lo):
            total = mm_ps.tile([P, PACK, BLK], F32, name="total", tag="turn")
            for t in range(PACK):
                nc.tensor.matmul(
                    total[:, t, :], ex[t][:, lo : lo + BLK], ident[:], start=(t == 0), stop=False, is_transpose=True
                )
            return total

        def add_neighbours(lo, totals, order):
            hi = lo + BLK * len(totals)
            for step, (on_scalar, t, which) in enumerate(order):
                terms, lst = looked_up[which]
                gather(on_scalar, terms[t][:, lo:hi], ex[t], lst, lo, hi)
                for b, total in enumerate(totals):
                    nc.tensor.matmul(
                        total[:, t, :],
                        terms[t][:, lo + b * BLK : lo + (b + 1) * BLK],
                        ident[:],
                        start=False,
                        stop=(step == len(order) - 1),
                        is_transpose=True,
                    )

        def split_by_tile(n_scalar):
            tiles = list(reversed(range(PACK - n_scalar, PACK))) + list(range(PACK - n_scalar))
            return [(t >= PACK - n_scalar, t, which) for t in tiles for which in range(2)]

        def invert(total):
            root_t = ring.tile([P, PACK, BLK], F32, name="root_t")
            nc.scalar.activation(out=root_t[:], in_=total[:], func=ACT.Abs_reciprocal_sqrt, scale=0.5)
            inv_t = ring.tile([P, PACK, BLK], F32, name="inv_t")
            nc.scalar.activation(out=inv_t[:], in_=root_t[:], func=ACT.Square)
            inv = back_ps.tile([P, PACK, BLK], F32, name="inv")
            for t in range(PACK):
                nc.tensor.transpose(inv[:, t, :], inv_t[:, t, :], ident[:])
            return inv

        def quantise_z(lo, invs):
            zb = held.tile([P, len(invs), BLK * PACK], BF16, name="zb%d" % lo, align_bytes=64)
            for b, inv in enumerate(invs):
                blk = slice(lo + b * BLK, lo + (b + 1) * BLK)
                nc.vector.tensor_tensor(
                    out=interleaved(zb[:, b, :]), in0=by_runs(exg[:, :, blk]), in1=by_runs(inv[:]), op=ALU.mult
                )
            cols = slice(lo, lo + BLK * len(invs))
            nc.vector.quantize_mx(
                out=zw[:, cols].bitcast(FP8X4), scales=zs[:, cols], in_=zb[:].rearrange("p b c -> p (b c)")
            )

        def second_layer(lo, hi, tag, bufs, n_scalar):
            banks = [mm_ps.tile([P, 2, hi - lo], F32, name="h2_ps", tag=tag, bufs=bufs) for pair in range(2)]
            for t in range(PACK):
                product(banks[t // 2][:, t % 2, :], w2w, w2s, t, zw[:, lo:hi], zs[:, lo:hi])
            for t in range(PACK):
                sums = banks[t // 2][:, t % 2, :]
                if t < n_scalar:
                    nc.scalar.activation(out=h2[t][:, lo:hi], in_=sums, func=ACT.Copy, scale=SIXTEENTH)
                else:
                    nc.vector.tensor_scalar(out=h2[t][:, lo:hi], in0=sums, scalar1=SIXTEENTH, scalar2=None, op0=ALU.mult)

        totals = [open_sum(lo) for lo in range(0, S, BLK)]
        add_neighbours(0, totals[0:1], [(which == 0, t, which) for t in range(PACK) for which in range(2)])
        inv0 = invert(totals[0])
        add_neighbours(BLK, totals[1:3], split_by_tile(1))
        inv1 = invert(totals[1])
        inv2 = invert(totals[2])
        add_neighbours(3 * BLK, totals[3:4], split_by_tile(2))
        inv3 = invert(totals[3])
        for t in range(PACK):
            nc.vector.tensor_scalar(
                out=exg[:, t, :], in0=ex[t][:], scalar1=gs_t[:, t : t + 1], scalar2=None, op0=ALU.mult
            )
        w2w = weight_words("w2", l_k2, "ex2")
        quantise_z(0, [inv0, inv1])
        second_layer(0, HALF, "first", 2, PACK)
        quantise_z(2 * BLK, [inv2])
        second_layer(2 * BLK, 3 * BLK, "turn", PACK, 2)
        quantise_z(3 * BLK, [inv3])
        second_layer(3 * BLK, S, "turn", PACK, 2)

        tile_order = (2, 0, 1, 3)
        g3 = [held.tile([P, S], F32, name="g3_%d" % t, tag="g3_%d" % t) for t in range(PACK)]
        st = [held.tile([P, S], F32, name="st%d" % t) for t in range(PACK)]
        for t in tile_order:
            for lo in range(0, S, HALF):
                on_vector = t == 2 or (t == 3 and lo == 0)
                gather(not on_vector, g3[t][:, lo : lo + HALF], h2[t], l_n3, lo, lo + HALF)
        for t in tile_order:
            nc.vector.tensor_tensor(out=st[t][:], in0=h2[t][:], in1=g3[t][:], op=ALU.max)

        res = held.tile([P, PACK, S], F32, name="res")
        ow = held.tile([P, S], I32, name="ow", align_bytes=64)
        osc = held.tile([P, S], U8, name="osc", align_bytes=64)
        out_rows = out_0.rearrange("(p t) j -> p t j", t=PACK)
        out_words = out_1[0].rearrange("p n t -> p (n t)").bitcast(I32)
        for lo, hi, slot in ((0, HALF, "g4"), (HALF, HALF + BLK, "g3_3"), (HALF + BLK, S, "g4")):
            g4 = held.tile([P, PACK, hi - lo], F32, name="g4", tag=slot)
            for t in tile_order:
                gather(True, g4[:, t, :], st[t], l_n4, lo, hi)
                nc.vector.tensor_tensor(out=res[:, t, lo:hi], in0=st[t][:, lo:hi], in1=g4[:, t, :], op=ALU.min)
            nc.sync.dma_start(out_rows[:, :, lo:hi], res[:, :, lo:hi])
            ob = held.tile([P, (hi - lo) * PACK], BF16, name="ob%d" % lo, align_bytes=64)
            nc.vector.tensor_copy(out=interleaved(ob[:]), in_=by_runs(res[:, :, lo:hi]))
            nc.vector.quantize_mx(out=ow[:, lo:hi].bitcast(FP8X4), scales=osc[:, lo:hi], in_=ob[:])
            nc.sync.dma_start(out_words[:, lo:hi], ow[:, lo:hi])
        out_scales = out_2[0].bitcast(I32)
        for j in range(4):
            queue = nc.sync if j % 2 else nc.scalar
            queue.dma_start(out_scales[j:SCALE_ROWS:4, :], osc[:].bitcast(I32)[j:P:QUADRANT, :])
